import numpy as np
import ml_dtypes


def mxq(x, axis, fmt="e4m3"):
    dtype, down = {"e4m3": (ml_dtypes.float8_e4m3fn, 7), "e5m2": (ml_dtypes.float8_e5m2, 14)}[fmt]
    v = np.moveaxis(np.asarray(x, np.float32).astype(ml_dtypes.bfloat16).astype(np.float64), axis, -1)
    blocks = v.reshape(v.shape[:-1] + (-1, 32))
    amax = np.abs(blocks).max(-1, keepdims=True)
    byte = np.maximum(np.where(amax > 0, np.frexp(amax)[1] - 1 + 127, 0) - down, 1)
    scale = np.exp2(byte - 127.0)
    codes = (blocks / scale).astype(np.float32).astype(dtype).astype(np.float64)
    return np.moveaxis((codes * scale).reshape(v.shape), -1, axis)


WIDE = False


def mx_kscale(k):
    if not WIDE:
        return np.ones(k)
    levels = np.array([10, -10, 5, -5, 0])
    if k % 512:
        return np.exp2(np.random.permutation(np.resize(levels, k // 32))).repeat(32)
    a = np.empty((k // 512, 16))
    for p in range(k // 512):
        a[p, :8] = np.random.permutation(np.resize(levels, 8))
        for g in range(8):
            far = levels[np.abs(levels - a[p, g]) >= 10]
            a[p, g + 8] = far[np.random.randint(len(far))]
    return np.exp2(a.ravel()).repeat(32)


def f64(x):
    return np.asarray(x).astype(np.float64)


def striped(idx):
    return np.tile(idx.reshape(-1, 16).T, (8, 1)).astype(np.uint16)


def unstriped(offs):
    return offs[:16].T.reshape(-1).astype(np.int64)


def striped8(idx):
    return np.concatenate([x.reshape(-1, 16).T for x in idx]).astype(np.uint16)


def runs(offs, k):
    lists = np.stack([offs[16 * r : 16 * r + 16].T.reshape(-1) for r in range(8)]).astype(np.int64)
    return lists[np.arange(k) % 512 // 64]


def pack_weight(w):
    k, n = w.shape
    w = f64(np.asarray(w, np.float32).astype(ml_dtypes.bfloat16)).reshape(k // 32, 32, n)
    amax = np.abs(w).max(1)
    byte = np.clip(np.where(amax > 0, np.frexp(amax)[1] - 1 + 127 - 7, 1), 1, 254)
    scaled = (w * np.exp2(127.0 - byte)[:, None, :]).reshape(k, n).astype(np.float32)
    words = np.ascontiguousarray(scaled.reshape(k // 512, 128, 4, n).transpose(0, 1, 3, 2)).astype(ml_dtypes.float8_e4m3fn).view(np.uint8)
    return words, np.ascontiguousarray(byte.astype(np.uint8).reshape(k // 512, 16, n))


def unpack_weight(words, scales):
    g, p, n, _ = words.shape
    vals = np.ascontiguousarray(words).view(ml_dtypes.float8_e4m3fn).astype(np.float64) * np.repeat(np.exp2(scales.astype(np.float64) - 127.0), 8, axis=1)[..., None]
    return vals.transpose(0, 1, 3, 2).reshape(g * 512, n)


def relu(v):
    return np.maximum(v, 0.0)


K, T, S, V, N, H = 512, 2048, 1024, 512, 512, 512


def setup_inputs():
    n = np.random.standard_normal
    s = mx_kscale(K)[:, None]
    u = mx_kscale(H)
    packed_xT = pack_weight(n((K, T)) * s)
    return {
        "x_words": packed_xT[0],
        "x_scales": packed_xT[1],
        "w1": (n((K, H)) / np.sqrt(K) / s * u).astype(np.float32),
        "w2": (n((H, H)) / np.sqrt(H) / u[:, None] * u).astype(np.float32),
        "res": n((N, S)).astype(np.float32),
        "w3": (n((H, N)) / np.sqrt(H) / u[:, None]).astype(np.float32),
        "offs": striped(np.random.permutation(T)[:S]),
        "l1": striped8(np.stack([np.random.permutation(S)[:V] for _ in range(8)])),
        "r1": striped8(np.stack([np.random.permutation(S)[:V] for _ in range(8)])),
        "par": striped8(np.random.randint(0, V, (8, S))),
    }


def reference(x_words, x_scales, w1, w2, res, w3, offs, l1, r1, par):
    xq = unpack_weight(x_words, x_scales)[:, unstriped(offs)]
    y = mxq(f64(w1), 0, "e4m3").T @ xq
    z = y[np.arange(H)[:, None], runs(l1, H)] + y[np.arange(H)[:, None], runs(r1, H)]
    h = relu(mxq(f64(w2), 0, "e4m3").T @ mxq(z, 0, "e4m3"))
    z2 = h[np.arange(H)[:, None], runs(par, H)] - (0.25 * y)
    return f64(res) + (mxq(f64(w3), 0, "e4m3").T @ mxq(z2, 0, "e4m3"))

@@ -1,0 +1,243 @@
+from contextlib import ExitStack
+
+import concourse.mybir as mybir
+
+F32 = mybir.dt.float32
+BF16 = mybir.dt.bfloat16
+I32 = mybir.dt.int32
+U32 = mybir.dt.uint32
+U16 = mybir.dt.uint16
+U8 = mybir.dt.uint8
+FP8X4 = mybir.dt.float8_e4m3fn_x4
+ADD = mybir.AluOpType.add
+COPY = mybir.ActivationFunctionType.Copy
+RELU = mybir.ActivationFunctionType.Relu
+
+P = 128
+K, T, S, V, N, H = 512, 2048, 1024, 512, 512, 512
+FLOPS = 2 * K * H * S + 2 * H * H * V + 2 * H * N * S
+HALF = 256
+X_CHUNKS = ((0, 512), (512, 256), (768, 256))
+OUT_CHUNKS = ((0, 256), (256, 256), (512, 256), (768, 128), (896, 128))
+Z_SPLIT = 192
+
+
+def tile_picked_inout_relu_p_kernel(
+    tc, x_words, x_scales, w1, w2, res, w3, offs, l1, r1, par, out
+):
+    nc = tc.nc
+    with ExitStack() as ctx:
+        keep = ctx.enter_context(tc.tile_pool(name="keep", bufs=1))
+        ring = ctx.enter_context(tc.tile_pool(name="ring", bufs=2))
+        psum = ctx.enter_context(tc.psum_pool(name="psum", bufs=8))
+
+        def entries(lst, first, count):
+            return lst[:, first // 16 : (first + count) // 16]
+
+        def load_half(w, half):
+            raw = ring.tile([P, 4, HALF], F32, name="raw")
+            nc.sync.dma_start(
+                out=raw[:],
+                in_=w.rearrange("(p j) c -> p j c", j=4)[:, :, half * HALF : (half + 1) * HALF],
+            )
+            return raw
+
+        def mx_pair(name, width):
+            codes = keep.tile([P, width], U32, name=name + "_codes", align_bytes=64)
+            scales = keep.tile([P, width], U8, name=name + "_scales", align_bytes=64)
+            return codes, scales
+
+        def quantize(pair, first, count, src):
+            nc.vector.quantize_mx(
+                out=pair[0][:, first : first + count].bitcast(FP8X4),
+                scales=pair[1][:, first : first + count],
+                in_=src,
+            )
+
+        def product(acc, w_pair, t, a_pair, first, count):
+            nc.tensor.matmul_mx(
+                out=acc,
+                lhsT=w_pair[0][:, t * P : (t + 1) * P].bitcast(FP8X4),
+                lhsT_scale=w_pair[1][:, t * P : (t + 1) * P],
+                rhs=a_pair[0][:, first : first + count].bitcast(FP8X4),
+                rhs_scale=a_pair[1][:, first : first + count],
+                start=True,
+                stop=True,
+            )
+
+        def weave_views(dst, src):
+            return dst.rearrange("p (c i) t -> p c t i", i=4), src.rearrange("p t (c i) -> p c t i", i=4)
+
+        offs_sb = keep.tile([P, S // 16], U16, name="offs_sb")
+        nc.sync.dma_start(offs_sb[:], offs)
+        scale_win = keep.tile([P, T], U8, name="scale_win", align_bytes=64)
+        nc.vector.memset(scale_win[:].bitcast(I32), 0)
+        for q in range(4):
+            nc.scalar.dma_start(
+                out=scale_win[32 * q : 32 * q + 4, :].bitcast(I32),
+                in_=x_scales[0, 4 * q : 4 * q + 4, :].bitcast(I32),
+            )
+        l1_sb = keep.tile([P, V // 16], U16, name="l1_sb")
+        nc.sync.dma_start(l1_sb[:], l1)
+        r1_sb = keep.tile([P, V // 16], U16, name="r1_sb")
+        nc.sync.dma_start(r1_sb[:], r1)
+        word_win = keep.tile([P, T], U32, name="word_win", align_bytes=64)
+        nc.sync.dma_start(
+            out=word_win[:].bitcast(I32),
+            in_=x_words[0].rearrange("p n t -> p (n t)").bitcast(I32),
+        )
+        w1_lo = load_half(w1, 0)
+        w1_hi = load_half(w1, 1)
+        par_sb = keep.tile([P, S // 16], U16, name="par_sb")
+        nc.sync.dma_start(par_sb[:], par)
+
+        x_mx = mx_pair("x", S)
+
+        def pick(sort, window, first, count):
+            nc.vector.tensor_copy(
+                x_mx[sort][:, first : first + count], window[:].indirect(entries(offs_sb, first, count))
+            )
+
+        def dealt_views(dst, raw, half, t0, t1):
+            m0 = half * (HALF // 4)
+            return (
+                dst[:, t0:t1, m0 : m0 + HALF // 4, :].rearrange("p t m j -> p m j t"),
+                raw[:].rearrange("p j (m t) -> p m j t", t=4)[:, :, :, t0:t1],
+            )
+
+        w1_bf = keep.tile([P, 4, P, 4], BF16, name="w1_bf", tag="early", align_bytes=64)
+        w1_mx = mx_pair("w1", H)
+        for half, raw in enumerate((w1_lo, w1_hi)):
+            o, i = dealt_views(w1_bf, raw, half, 0, 4)
+            nc.scalar.copy(o, i)
+            pick(0, word_win, half * 512, 512)
+        pick(1, scale_win, *X_CHUNKS[0])
+        quantize(w1_mx, 0, P, w1_bf[:, 0].rearrange("p m j -> p (m j)"))
+        for first, count in X_CHUNKS[1:]:
+            pick(1, scale_win, first, count)
+
+        quarter = [keep.tile([P, S], F32, name=f"quarter{t}") for t in range(4)]
+
+        def first_layer(t, chunks):
+            for first, count in chunks:
+                acc = psum.tile([P, 512], F32, name="acc")
+                product(acc[:, :count], w1_mx, t, x_mx, first, count)
+                nc.scalar.activation(quarter[t][:, first : first + count], acc[:, :count], COPY, scale=-0.25)
+
+        first_layer(0, X_CHUNKS)
+        for t in range(1, 4):
+            quantize(w1_mx, t * P, P, w1_bf[:, t].rearrange("p m j -> p (m j)"))
+        for t in range(1, 4):
+            first_layer(t, ((0, 512), (512, 512)))
+
+        w2_bf = keep.tile([P, 4, P, 4], BF16, name="w2_bf", tag="late", align_bytes=64)
+        w2_mx = mx_pair("w2", H)
+        for half in range(2):
+            raw = load_half(w2, half)
+            o, i = dealt_views(w2_bf, raw, half, 0, 4)
+            nc.scalar.copy(o, i)
+        res_view = res.rearrange("(t p) s -> p t s", p=P)
+        out_view = out.rearrange("(t p) s -> p t s", p=P)
+        res_lo = keep.tile([P, 4, 512], F32, name="res_lo", tag="early", align_bytes=64)
+        nc.sync.dma_start(out=res_lo[:], in_=res_view[:, :, 0:512])
+        w3_bf = keep.tile([P, N, 4], BF16, name="w3_bf", align_bytes=64)
+        w3_mx = mx_pair("w3", N)
+        w3_raw = [load_half(w3, half) for half in range(2)]
+
+        left = [keep.tile([P, V], F32, name=f"left{t}") for t in range(4)]
+        z_sum = [keep.tile([P, 4, HALF], F32, name=f"z_sum{c}") for c in range(2)]
+        z_bf = [keep.tile([P, HALF, 4], BF16, name=f"z_bf{c}", align_bytes=64) for c in range(2)]
+        z_mx = mx_pair("z", V)
+        hidden = [keep.tile([P, V], F32, name=f"hidden{t}") for t in range(4)]
+
+        def gather_left(t):
+            nc.vector.tensor_copy(left[t][:], quarter[t][:].indirect(l1_sb[:]))
+
+        def add_right(t, c):
+            nc.vector.tensor_tensor(
+                z_sum[c][:, t, :],
+                quarter[t][:].indirect(entries(r1_sb, c * HALF, HALF)),
+                left[t][:, c * HALF : (c + 1) * HALF],
+                ADD,
+            )
+
+        def second_layer(c):
+            for t in range(4):
+                acc = psum.tile([P, 512], F32, name="acc")
+                product(acc[:, :HALF], w2_mx, t, z_mx, c * HALF, HALF)
+                nc.scalar.activation(hidden[t][:, c * HALF : (c + 1) * HALF], acc[:, :HALF], RELU)
+
+        gather_left(0)
+        for t in range(1, 4):
+            gather_left(t)
+            add_right(t - 1, 0)
+        quantize(w2_mx, 0, H, w2_bf[:].rearrange("p t m j -> p (t m j)"))
+        add_right(3, 0)
+        res_hi = keep.tile([P, 4, 512], F32, name="res_hi", tag="late", align_bytes=64)
+        nc.sync.dma_start(out=res_hi[:], in_=res_view[:, :, 512:1024])
+        o, i = weave_views(z_bf[0][:], z_sum[0][:])
+        nc.scalar.activation(o, i, COPY, scale=-4.0)
+        add_right(0, 1)
+        add_right(1, 1)
+        quantize(z_mx, 0, HALF, z_bf[0][:].rearrange("p v t -> p (v t)"))
+        second_layer(0)
+        add_right(2, 1)
+        add_right(3, 1)
+        o, i = weave_views(z_bf[1][:, Z_SPLIT:, :], z_sum[1][:, :, Z_SPLIT:])
+        nc.scalar.activation(o, i, COPY, scale=-4.0)
+        o, i = weave_views(z_bf[1][:, :Z_SPLIT, :], z_sum[1][:, :, :Z_SPLIT])
+        nc.vector.tensor_scalar_mul(o, i, -4.0)
+        quantize(z_mx, HALF, HALF, z_bf[1][:].rearrange("p v t -> p (v t)"))
+        second_layer(1)
+        for half in range(2):
+            o, i = weave_views(w3_bf[:, half * HALF : (half + 1) * HALF, :], w3_raw[half][:])
+            nc.scalar.copy(o, i)
+        quantize(w3_mx, 0, N, w3_bf[:].rearrange("p n j -> p (n j)"))
+
+        z2_mx = mx_pair("z2", S)
+
+        def gather_parents(first, count):
+            z2_sum = ring.tile([P, 4, count], F32, name="z2_sum")
+            for t in range(4):
+                nc.vector.tensor_tensor(
+                    z2_sum[:, t, :],
+                    hidden[t][:].indirect(entries(par_sb, first, count)),
+                    quarter[t][:, first : first + count],
+                    ADD,
+                )
+            z2_bf = ring.tile([P, count, 4], BF16, name="z2_bf", align_bytes=64)
+            o, i = weave_views(z2_bf[:], z2_sum[:])
+            nc.scalar.copy(o, i)
+            return z2_bf
+
+        def third_layer(first, count, z2_bf):
+            quantize(z2_mx, first, count, z2_bf[:].rearrange("p s t -> p (s t)"))
+            per_bank = 512 // count
+            banks = []
+            for t0 in range(0, 4, per_bank):
+                acc = psum.tile([P, per_bank, count], F32, name="acc")
+                for t in range(t0, t0 + per_bank):
+                    product(acc[:, t - t0, :], w3_mx, t, z2_mx, first, count)
+                banks.append(acc)
+            return banks
+
+        def finish(first, count, banks):
+            per_bank = 512 // count
+            res_sb = res_lo if first < 512 else res_hi
+            col = first % 512
+            result = ring.tile([P, 4, count], F32, name="result")
+            for b, acc in enumerate(banks):
+                rows = slice(b * per_bank, (b + 1) * per_bank)
+                nc.vector.tensor_tensor(result[:, rows, :], acc[:], res_sb[:, rows, col : col + count], ADD)
+            nc.sync.dma_start(out=out_view[:, :, first : first + count], in_=result[:])
+
+        woven = {}
+        banks = {}
+        n_chunks = len(OUT_CHUNKS)
+        for step in range(n_chunks + 2):
+            if step < n_chunks:
+                woven[step] = gather_parents(*OUT_CHUNKS[step])
+            if step >= 2:
+                finish(*OUT_CHUNKS[step - 2], banks[step - 2])
+            if 1 <= step <= n_chunks:
+                banks[step - 1] = third_layer(*OUT_CHUNKS[step - 1], woven[step - 1])

@@ -19,7 +19,6 @@ FLOPS = 2 * K * H * S + 2 * H * H * V + 2 * H * N * S
 HALF = 256
 X_CHUNKS = ((0, 512), (512, 256), (768, 256))
 OUT_CHUNKS = ((0, 256), (256, 256), (512, 256), (768, 128), (896, 128))
-Z_SPLIT = 192
 
 
 def tile_picked_inout_relu_p_kernel(
@@ -34,16 +33,13 @@ def tile_picked_inout_relu_p_kernel(
         def entries(lst, first, count):
             return lst[:, first // 16 : (first + count) // 16]
 
-        def load_half(w, half):
-            raw = ring.tile([P, 4, HALF], F32, name="raw")
-            nc.sync.dma_start(
-                out=raw[:],
-                in_=w.rearrange("(p j) c -> p j c", j=4)[:, :, half * HALF : (half + 1) * HALF],
-            )
+        def load_weight(w, name, tag):
+            raw = keep.tile([P, 4, 512], F32, name=name, tag=tag, align_bytes=64)
+            nc.sync.dma_start(out=raw[:], in_=w.rearrange("(p j) c -> p j c", j=4))
             return raw
 
-        def mx_pair(name, width):
-            codes = keep.tile([P, width], U32, name=name + "_codes", align_bytes=64)
+        def mx_pair(name, width, tag=None):
+            codes = keep.tile([P, width], U32, name=name + "_codes", tag=tag or name + "_codes", align_bytes=64)
             scales = keep.tile([P, width], U8, name=name + "_scales", align_bytes=64)
             return codes, scales
 
@@ -54,13 +50,13 @@ def tile_picked_inout_relu_p_kernel(
                 in_=src,
             )
 
-        def product(acc, w_pair, t, a_pair, first, count):
+        def product(acc, w_pair, t, codes, scales):
             nc.tensor.matmul_mx(
                 out=acc,
                 lhsT=w_pair[0][:, t * P : (t + 1) * P].bitcast(FP8X4),
                 lhsT_scale=w_pair[1][:, t * P : (t + 1) * P],
-                rhs=a_pair[0][:, first : first + count].bitcast(FP8X4),
-                rhs_scale=a_pair[1][:, first : first + count],
+                rhs=codes.bitcast(FP8X4),
+                rhs_scale=scales,
                 start=True,
                 stop=True,
             )
@@ -70,134 +66,128 @@ def tile_picked_inout_relu_p_kernel(
 
         offs_sb = keep.tile([P, S // 16], U16, name="offs_sb")
         nc.sync.dma_start(offs_sb[:], offs)
-        scale_win = keep.tile([P, T], U8, name="scale_win", align_bytes=64)
-        nc.vector.memset(scale_win[:].bitcast(I32), 0)
-        for q in range(4):
-            nc.scalar.dma_start(
-                out=scale_win[32 * q : 32 * q + 4, :].bitcast(I32),
-                in_=x_scales[0, 4 * q : 4 * q + 4, :].bitcast(I32),
-            )
-        l1_sb = keep.tile([P, V // 16], U16, name="l1_sb")
-        nc.sync.dma_start(l1_sb[:], l1)
-        r1_sb = keep.tile([P, V // 16], U16, name="r1_sb")
-        nc.sync.dma_start(r1_sb[:], r1)
+        scale_rows = keep.tile([P, T // 4], I32, name="scale_rows")
+        for r in range(4):
+            nc.sync.dma_start(out=scale_rows[r:P:32, :], in_=x_scales[0, r:16:4, :].bitcast(I32))
+        w1_raw = load_weight(w1, "w1_raw", "stage_a")
         word_win = keep.tile([P, T], U32, name="word_win", align_bytes=64)
         nc.sync.dma_start(
             out=word_win[:].bitcast(I32),
             in_=x_words[0].rearrange("p n t -> p (n t)").bitcast(I32),
         )
-        w1_lo = load_half(w1, 0)
-        w1_hi = load_half(w1, 1)
+        l1_sb = keep.tile([P, V // 16], U16, name="l1_sb")
+        nc.sync.dma_start(l1_sb[:], l1)
+        r1_sb = keep.tile([P, V // 16], U16, name="r1_sb")
+        nc.sync.dma_start(r1_sb[:], r1)
         par_sb = keep.tile([P, S // 16], U16, name="par_sb")
         nc.sync.dma_start(par_sb[:], par)
+        scale_win = keep.tile([P, T], U8, name="scale_win", align_bytes=64)
+        nc.vector.memset(scale_win[:].bitcast(I32), 0)
+        for q in range(4):
+            nc.vector.tensor_copy(scale_win[32 * q : 32 * q + 4, :].bitcast(I32), scale_rows[32 * q : 32 * q + 4, :])
 
-        x_mx = mx_pair("x", S)
+        x_bytes = keep.tile([P, S], U8, name="x_bytes", align_bytes=64)
 
-        def pick(sort, window, first, count):
-            nc.vector.tensor_copy(
-                x_mx[sort][:, first : first + count], window[:].indirect(entries(offs_sb, first, count))
-            )
+        def pick(dst, window, first, count):
+            nc.vector.tensor_copy(dst, window[:].indirect(entries(offs_sb, first, count)))
 
-        def dealt_views(dst, raw, half, t0, t1):
+        def deal(dst, raw, half, t0, t1):
             m0 = half * (HALF // 4)
-            return (
-                dst[:, t0:t1, m0 : m0 + HALF // 4, :].rearrange("p t m j -> p m j t"),
-                raw[:].rearrange("p j (m t) -> p m j t", t=4)[:, :, :, t0:t1],
+            nc.scalar.copy(
+                dst[:, :, m0 : m0 + HALF // 4, :].rearrange("p t m j -> p m j t"),
+                raw[:].rearrange("p j (m t) -> p m j t", t=4)[:, m0 : m0 + HALF // 4, :, t0:t1],
             )
 
-        w1_bf = keep.tile([P, 4, P, 4], BF16, name="w1_bf", tag="early", align_bytes=64)
+        w1_first = keep.tile([P, 1, P, 4], BF16, name="w1_first", align_bytes=64)
+        w1_rest = keep.tile([P, 3, P, 4], BF16, name="w1_rest", tag="stage_b", align_bytes=64)
         w1_mx = mx_pair("w1", H)
-        for half, raw in enumerate((w1_lo, w1_hi)):
-            o, i = dealt_views(w1_bf, raw, half, 0, 4)
-            nc.scalar.copy(o, i)
-            pick(0, word_win, half * 512, 512)
-        pick(1, scale_win, *X_CHUNKS[0])
-        quantize(w1_mx, 0, P, w1_bf[:, 0].rearrange("p m j -> p (m j)"))
-        for first, count in X_CHUNKS[1:]:
-            pick(1, scale_win, first, count)
+        for dst, t0, t1 in ((w1_first, 0, 1), (w1_rest, 1, 4)):
+            for half in range(2):
+                deal(dst, w1_raw, half, t0, t1)
+        pick(x_bytes[:], scale_win, 0, S)
+        quantize(w1_mx, 0, P, w1_first[:].rearrange("p t m j -> p (t m j)"))
+        x_codes = []
+        for first, count in X_CHUNKS:
+            x_codes.append(keep.tile([P, count], U32, name=f"x_codes{first}", tag=f"x_codes{first}", align_bytes=64))
+            pick(x_codes[-1][:], word_win, first, count)
 
         quarter = [keep.tile([P, S], F32, name=f"quarter{t}") for t in range(4)]
 
-        def first_layer(t, chunks):
-            for first, count in chunks:
+        def first_layer(t, banks):
+            for chunks in banks:
                 acc = psum.tile([P, 512], F32, name="acc")
-                product(acc[:, :count], w1_mx, t, x_mx, first, count)
-                nc.scalar.activation(quarter[t][:, first : first + count], acc[:, :count], COPY, scale=-0.25)
+                start = X_CHUNKS[chunks[0]][0]
+                for c in chunks:
+                    first, count = X_CHUNKS[c]
+                    end = first + count
+                    product(acc[:, first - start : end - start], w1_mx, t, x_codes[c][:], x_bytes[:, first:end])
+                nc.scalar.activation(quarter[t][:, start:end], acc[:, : end - start], COPY, scale=-0.25)
 
-        first_layer(0, X_CHUNKS)
+        first_layer(0, ((0,), (1,), (2,)))
         for t in range(1, 4):
-            quantize(w1_mx, t * P, P, w1_bf[:, t].rearrange("p m j -> p (m j)"))
+            quantize(w1_mx, t * P, P, w1_rest[:, t - 1].rearrange("p m j -> p (m j)"))
         for t in range(1, 4):
-            first_layer(t, ((0, 512), (512, 512)))
+            first_layer(t, ((0,), (1, 2)))
 
-        w2_bf = keep.tile([P, 4, P, 4], BF16, name="w2_bf", tag="late", align_bytes=64)
-        w2_mx = mx_pair("w2", H)
+        w2_bf = keep.tile([P, 4, P, 4], BF16, name="w2_bf", tag="z_bf1", align_bytes=64)
+        w2_mx = mx_pair("w2", H, tag="w2_codes")
+        w2_raw = load_weight(w2, "w2_raw", "stage_a")
         for half in range(2):
-            raw = load_half(w2, half)
-            o, i = dealt_views(w2_bf, raw, half, 0, 4)
+            deal(w2_bf, w2_raw, half, 0, 4)
+        w3_raw = load_weight(w3, "w3_raw", "stage_b")
+        w3_bf = keep.tile([P, N, 4], BF16, name="w3_bf", align_bytes=64)
+        for half in range(2):
+            cols = slice(half * HALF, (half + 1) * HALF)
+            o, i = weave_views(w3_bf[:, cols, :], w3_raw[:, :, cols])
             nc.scalar.copy(o, i)
         res_view = res.rearrange("(t p) s -> p t s", p=P)
         out_view = out.rearrange("(t p) s -> p t s", p=P)
-        res_lo = keep.tile([P, 4, 512], F32, name="res_lo", tag="early", align_bytes=64)
+        res_lo = keep.tile([P, 4, 512], F32, name="res_lo", tag="stage_a", align_bytes=64)
         nc.sync.dma_start(out=res_lo[:], in_=res_view[:, :, 0:512])
-        w3_bf = keep.tile([P, N, 4], BF16, name="w3_bf", align_bytes=64)
-        w3_mx = mx_pair("w3", N)
-        w3_raw = [load_half(w3, half) for half in range(2)]
+        res_hi = keep.tile([P, 4, 512], F32, name="res_hi", tag="x_codes0", align_bytes=64)
+        nc.sync.dma_start(out=res_hi[:], in_=res_view[:, :, 512:1024])
 
         left = [keep.tile([P, V], F32, name=f"left{t}") for t in range(4)]
         z_sum = [keep.tile([P, 4, HALF], F32, name=f"z_sum{c}") for c in range(2)]
-        z_bf = [keep.tile([P, HALF, 4], BF16, name=f"z_bf{c}", align_bytes=64) for c in range(2)]
-        z_mx = mx_pair("z", V)
+        z_bf = [keep.tile([P, HALF, 4], BF16, name=f"z_bf{c}", tag=("stage_b", "z_bf1")[c], align_bytes=64) for c in range(2)]
         hidden = [keep.tile([P, V], F32, name=f"hidden{t}") for t in range(4)]
 
-        def gather_left(t):
-            nc.vector.tensor_copy(left[t][:], quarter[t][:].indirect(l1_sb[:]))
-
-        def add_right(t, c):
-            nc.vector.tensor_tensor(
-                z_sum[c][:, t, :],
-                quarter[t][:].indirect(entries(r1_sb, c * HALF, HALF)),
-                left[t][:, c * HALF : (c + 1) * HALF],
-                ADD,
-            )
-
-        def second_layer(c):
-            for t in range(4):
-                acc = psum.tile([P, 512], F32, name="acc")
-                product(acc[:, :HALF], w2_mx, t, z_mx, c * HALF, HALF)
-                nc.scalar.activation(hidden[t][:, c * HALF : (c + 1) * HALF], acc[:, :HALF], RELU)
-
-        gather_left(0)
-        for t in range(1, 4):
-            gather_left(t)
-            add_right(t - 1, 0)
+        for t in range(4):
+            for c in range(2):
+                nc.vector.tensor_copy(
+                    left[t][:, c * HALF : (c + 1) * HALF], quarter[t][:].indirect(entries(l1_sb, c * HALF, HALF))
+                )
+            for c in range(2):
+                nc.vector.tensor_tensor(
+                    z_sum[c][:, t, :],
+                    quarter[t][:].indirect(entries(r1_sb, c * HALF, HALF)),
+                    left[t][:, c * HALF : (c + 1) * HALF],
+                    ADD,
+                )
         quantize(w2_mx, 0, H, w2_bf[:].rearrange("p t m j -> p (t m j)"))
-        add_right(3, 0)
-        res_hi = keep.tile([P, 4, 512], F32, name="res_hi", tag="late", align_bytes=64)
-        nc.sync.dma_start(out=res_hi[:], in_=res_view[:, :, 512:1024])
         o, i = weave_views(z_bf[0][:], z_sum[0][:])
         nc.scalar.activation(o, i, COPY, scale=-4.0)
-        add_right(0, 1)
-        add_right(1, 1)
-        quantize(z_mx, 0, HALF, z_bf[0][:].rearrange("p v t -> p (v t)"))
-        second_layer(0)
-        add_right(2, 1)
-        add_right(3, 1)
-        o, i = weave_views(z_bf[1][:, Z_SPLIT:, :], z_sum[1][:, :, Z_SPLIT:])
-        nc.scalar.activation(o, i, COPY, scale=-4.0)
-        o, i = weave_views(z_bf[1][:, :Z_SPLIT, :], z_sum[1][:, :, :Z_SPLIT])
+        o, i = weave_views(z_bf[1][:], z_sum[1][:])
         nc.vector.tensor_scalar_mul(o, i, -4.0)
-        quantize(z_mx, HALF, HALF, z_bf[1][:].rearrange("p v t -> p (v t)"))
-        second_layer(1)
-        for half in range(2):
-            o, i = weave_views(w3_bf[:, half * HALF : (half + 1) * HALF, :], w3_raw[half][:])
-            nc.scalar.copy(o, i)
+        z_mx = []
+        for c in range(2):
+            z_mx.append(mx_pair(f"z{c}", HALF, tag="stage_b" if c else None))
+            quantize(z_mx[c], 0, HALF, z_bf[c][:].rearrange("p v t -> p (v t)"))
+        for t in range(4):
+            for c in range(2):
+                acc = psum.tile([P, 512], F32, name="acc")
+                product(acc[:, :HALF], w2_mx, t, z_mx[c][0][:], z_mx[c][1][:])
+                nc.scalar.activation(hidden[t][:, c * HALF : (c + 1) * HALF], acc[:, :HALF], RELU)
+        w3_mx = mx_pair("w3", N, tag="z_bf1")
         quantize(w3_mx, 0, N, w3_bf[:].rearrange("p n j -> p (n j)"))
 
         z2_mx = mx_pair("z2", S)
 
         def gather_parents(first, count):
-            z2_sum = ring.tile([P, 4, count], F32, name="z2_sum")
+            if first == 512:
+                z2_sum = keep.tile([P, 4, count], F32, name="z2_third", tag="w2_codes", align_bytes=64)
+            else:
+                z2_sum = ring.tile([P, 4, count], F32, name="z2_sum")
             for t in range(4):
                 nc.vector.tensor_tensor(
                     z2_sum[:, t, :],
@@ -212,24 +202,32 @@ def tile_picked_inout_relu_p_kernel(
 
         def third_layer(first, count, z2_bf):
             quantize(z2_mx, first, count, z2_bf[:].rearrange("p s t -> p (s t)"))
-            per_bank = 512 // count
+            per_bank = 2 if first + count == S else 512 // count
             banks = []
             for t0 in range(0, 4, per_bank):
                 acc = psum.tile([P, per_bank, count], F32, name="acc")
                 for t in range(t0, t0 + per_bank):
-                    product(acc[:, t - t0, :], w3_mx, t, z2_mx, first, count)
+                    product(
+                        acc[:, t - t0, :],
+                        w3_mx,
+                        t,
+                        z2_mx[0][:, first : first + count],
+                        z2_mx[1][:, first : first + count],
+                    )
                 banks.append(acc)
             return banks
 
         def finish(first, count, banks):
-            per_bank = 512 // count
+            last = first + count == S
+            per_bank = 2 if last else 512 // count
             res_sb = res_lo if first < 512 else res_hi
             col = first % 512
-            result = ring.tile([P, 4, count], F32, name="result")
+            result = keep.tile([P, 4, count], F32, name=f"result{first}")
             for b, acc in enumerate(banks):
                 rows = slice(b * per_bank, (b + 1) * per_bank)
                 nc.vector.tensor_tensor(result[:, rows, :], acc[:], res_sb[:, rows, col : col + count], ADD)
-            nc.sync.dma_start(out=out_view[:, :, first : first + count], in_=result[:])
+                queue = nc.scalar if b and last else nc.sync
+                queue.dma_start(out=out_view[:, rows, first : first + count], in_=result[:, rows, :])
 
         woven = {}
         banks = {}
@@ -237,7 +235,7 @@ def tile_picked_inout_relu_p_kernel(
         for step in range(n_chunks + 2):
             if step < n_chunks:
                 woven[step] = gather_parents(*OUT_CHUNKS[step])
-            if step >= 2:
-                finish(*OUT_CHUNKS[step - 2], banks[step - 2])
             if 1 <= step <= n_chunks:
                 banks[step - 1] = third_layer(*OUT_CHUNKS[step - 1], woven[step - 1])
+            if step >= 2:
+                finish(*OUT_CHUNKS[step - 2], banks[step - 2])

from contextlib import ExitStack

import concourse.mybir as mybir

F32 = mybir.dt.float32
BF16 = mybir.dt.bfloat16
I32 = mybir.dt.int32
U32 = mybir.dt.uint32
U16 = mybir.dt.uint16
U8 = mybir.dt.uint8
FP8X4 = mybir.dt.float8_e4m3fn_x4
ADD = mybir.AluOpType.add
COPY = mybir.ActivationFunctionType.Copy
RELU = mybir.ActivationFunctionType.Relu

P = 128
K, T, S, V, N, H = 512, 2048, 1024, 512, 512, 512
FLOPS = 2 * K * H * S + 2 * H * H * V + 2 * H * N * S
HALF = 256
X_CHUNKS = ((0, 512), (512, 256), (768, 256))
OUT_CHUNKS = ((0, 256), (256, 256), (512, 256), (768, 128), (896, 128))


def tile_picked_inout_relu_p_kernel(
    tc, x_words, x_scales, w1, w2, res, w3, offs, l1, r1, par, out
):
    nc = tc.nc
    with ExitStack() as ctx:
        keep = ctx.enter_context(tc.tile_pool(name="keep", bufs=1))
        ring = ctx.enter_context(tc.tile_pool(name="ring", bufs=2))
        psum = ctx.enter_context(tc.psum_pool(name="psum", bufs=8))

        def entries(lst, first, count):
            return lst[:, first // 16 : (first + count) // 16]

        def load_weight(w, name, tag):
            raw = keep.tile([P, 4, 512], F32, name=name, tag=tag, align_bytes=64)
            nc.sync.dma_start(out=raw[:], in_=w.rearrange("(p j) c -> p j c", j=4))
            return raw

        def mx_pair(name, width, tag=None):
            codes = keep.tile([P, width], U32, name=name + "_codes", tag=tag or name + "_codes", align_bytes=64)
            scales = keep.tile([P, width], U8, name=name + "_scales", align_bytes=64)
            return codes, scales

        def quantize(pair, first, count, src):
            nc.vector.quantize_mx(
                out=pair[0][:, first : first + count].bitcast(FP8X4),
                scales=pair[1][:, first : first + count],
                in_=src,
            )

        def product(acc, w_pair, t, codes, scales):
            nc.tensor.matmul_mx(
                out=acc,
                lhsT=w_pair[0][:, t * P : (t + 1) * P].bitcast(FP8X4),
                lhsT_scale=w_pair[1][:, t * P : (t + 1) * P],
                rhs=codes.bitcast(FP8X4),
                rhs_scale=scales,
                start=True,
                stop=True,
            )

        def weave_views(dst, src):
            return dst.rearrange("p (c i) t -> p c t i", i=4), src.rearrange("p t (c i) -> p c t i", i=4)

        offs_sb = keep.tile([P, S // 16], U16, name="offs_sb")
        nc.sync.dma_start(offs_sb[:], offs)
        scale_rows = keep.tile([P, T // 4], I32, name="scale_rows")
        for r in range(4):
            nc.sync.dma_start(out=scale_rows[r:P:32, :], in_=x_scales[0, r:16:4, :].bitcast(I32))
        w1_raw = load_weight(w1, "w1_raw", "stage_a")
        word_win = keep.tile([P, T], U32, name="word_win", align_bytes=64)
        nc.sync.dma_start(
            out=word_win[:].bitcast(I32),
            in_=x_words[0].rearrange("p n t -> p (n t)").bitcast(I32),
        )
        l1_sb = keep.tile([P, V // 16], U16, name="l1_sb")
        nc.sync.dma_start(l1_sb[:], l1)
        r1_sb = keep.tile([P, V // 16], U16, name="r1_sb")
        nc.sync.dma_start(r1_sb[:], r1)
        par_sb = keep.tile([P, S // 16], U16, name="par_sb")
        nc.sync.dma_start(par_sb[:], par)
        scale_win = keep.tile([P, T], U8, name="scale_win", align_bytes=64)
        nc.vector.memset(scale_win[:].bitcast(I32), 0)
        for q in range(4):
            nc.vector.tensor_copy(scale_win[32 * q : 32 * q + 4, :].bitcast(I32), scale_rows[32 * q : 32 * q + 4, :])

        x_bytes = keep.tile([P, S], U8, name="x_bytes", align_bytes=64)

        def pick(dst, window, first, count):
            nc.vector.tensor_copy(dst, window[:].indirect(entries(offs_sb, first, count)))

        def deal(dst, raw, half, t0, t1):
            m0 = half * (HALF // 4)
            nc.scalar.copy(
                dst[:, :, m0 : m0 + HALF // 4, :].rearrange("p t m j -> p m j t"),
                raw[:].rearrange("p j (m t) -> p m j t", t=4)[:, m0 : m0 + HALF // 4, :, t0:t1],
            )

        w1_first = keep.tile([P, 1, P, 4], BF16, name="w1_first", align_bytes=64)
        w1_rest = keep.tile([P, 3, P, 4], BF16, name="w1_rest", tag="stage_b", align_bytes=64)
        w1_mx = mx_pair("w1", H)
        for dst, t0, t1 in ((w1_first, 0, 1), (w1_rest, 1, 4)):
            for half in range(2):
                deal(dst, w1_raw, half, t0, t1)
        pick(x_bytes[:], scale_win, 0, S)
        quantize(w1_mx, 0, P, w1_first[:].rearrange("p t m j -> p (t m j)"))
        x_codes = []
        for first, count in X_CHUNKS:
            x_codes.append(keep.tile([P, count], U32, name=f"x_codes{first}", tag=f"x_codes{first}", align_bytes=64))
            pick(x_codes[-1][:], word_win, first, count)

        quarter = [keep.tile([P, S], F32, name=f"quarter{t}") for t in range(4)]

        def first_layer(t, banks):
            for chunks in banks:
                acc = psum.tile([P, 512], F32, name="acc")
                start = X_CHUNKS[chunks[0]][0]
                for c in chunks:
                    first, count = X_CHUNKS[c]
                    end = first + count
                    product(acc[:, first - start : end - start], w1_mx, t, x_codes[c][:], x_bytes[:, first:end])
                nc.scalar.activation(quarter[t][:, start:end], acc[:, : end - start], COPY, scale=-0.25)

        first_layer(0, ((0,), (1,), (2,)))
        for t in range(1, 4):
            quantize(w1_mx, t * P, P, w1_rest[:, t - 1].rearrange("p m j -> p (m j)"))
        for t in range(1, 4):
            first_layer(t, ((0,), (1, 2)))

        w2_bf = keep.tile([P, 4, P, 4], BF16, name="w2_bf", tag="z_bf1", align_bytes=64)
        w2_mx = mx_pair("w2", H, tag="w2_codes")
        w2_raw = load_weight(w2, "w2_raw", "stage_a")
        for half in range(2):
            deal(w2_bf, w2_raw, half, 0, 4)
        w3_raw = load_weight(w3, "w3_raw", "stage_b")
        w3_bf = keep.tile([P, N, 4], BF16, name="w3_bf", align_bytes=64)
        for half in range(2):
            cols = slice(half * HALF, (half + 1) * HALF)
            o, i = weave_views(w3_bf[:, cols, :], w3_raw[:, :, cols])
            nc.scalar.copy(o, i)
        res_view = res.rearrange("(t p) s -> p t s", p=P)
        out_view = out.rearrange("(t p) s -> p t s", p=P)
        res_lo = keep.tile([P, 4, 512], F32, name="res_lo", tag="stage_a", align_bytes=64)
        nc.sync.dma_start(out=res_lo[:], in_=res_view[:, :, 0:512])
        res_hi = keep.tile([P, 4, 512], F32, name="res_hi", tag="x_codes0", align_bytes=64)
        nc.sync.dma_start(out=res_hi[:], in_=res_view[:, :, 512:1024])

        left = [keep.tile([P, V], F32, name=f"left{t}") for t in range(4)]
        z_sum = [keep.tile([P, 4, HALF], F32, name=f"z_sum{c}") for c in range(2)]
        z_bf = [keep.tile([P, HALF, 4], BF16, name=f"z_bf{c}", tag=("stage_b", "z_bf1")[c], align_bytes=64) for c in range(2)]
        hidden = [keep.tile([P, V], F32, name=f"hidden{t}") for t in range(4)]

        for t in range(4):
            for c in range(2):
                nc.vector.tensor_copy(
                    left[t][:, c * HALF : (c + 1) * HALF], quarter[t][:].indirect(entries(l1_sb, c * HALF, HALF))
                )
            for c in range(2):
                nc.vector.tensor_tensor(
                    z_sum[c][:, t, :],
                    quarter[t][:].indirect(entries(r1_sb, c * HALF, HALF)),
                    left[t][:, c * HALF : (c + 1) * HALF],
                    ADD,
                )
        quantize(w2_mx, 0, H, w2_bf[:].rearrange("p t m j -> p (t m j)"))
        o, i = weave_views(z_bf[0][:], z_sum[0][:])
        nc.scalar.activation(o, i, COPY, scale=-4.0)
        o, i = weave_views(z_bf[1][:], z_sum[1][:])
        nc.vector.tensor_scalar_mul(o, i, -4.0)
        z_mx = []
        for c in range(2):
            z_mx.append(mx_pair(f"z{c}", HALF, tag="stage_b" if c else None))
            quantize(z_mx[c], 0, HALF, z_bf[c][:].rearrange("p v t -> p (v t)"))
        for t in range(4):
            for c in range(2):
                acc = psum.tile([P, 512], F32, name="acc")
                product(acc[:, :HALF], w2_mx, t, z_mx[c][0][:], z_mx[c][1][:])
                nc.scalar.activation(hidden[t][:, c * HALF : (c + 1) * HALF], acc[:, :HALF], RELU)
        w3_mx = mx_pair("w3", N, tag="z_bf1")
        quantize(w3_mx, 0, N, w3_bf[:].rearrange("p n j -> p (n j)"))

        z2_mx = mx_pair("z2", S)

        def gather_parents(first, count):
            if first == 512:
                z2_sum = keep.tile([P, 4, count], F32, name="z2_third", tag="w2_codes", align_bytes=64)
            else:
                z2_sum = ring.tile([P, 4, count], F32, name="z2_sum")
            for t in range(4):
                nc.vector.tensor_tensor(
                    z2_sum[:, t, :],
                    hidden[t][:].indirect(entries(par_sb, first, count)),
                    quarter[t][:, first : first + count],
                    ADD,
                )
            z2_bf = ring.tile([P, count, 4], BF16, name="z2_bf", align_bytes=64)
            o, i = weave_views(z2_bf[:], z2_sum[:])
            nc.scalar.copy(o, i)
            return z2_bf

        def third_layer(first, count, z2_bf):
            quantize(z2_mx, first, count, z2_bf[:].rearrange("p s t -> p (s t)"))
            per_bank = 2 if first + count == S else 512 // count
            banks = []
            for t0 in range(0, 4, per_bank):
                acc = psum.tile([P, per_bank, count], F32, name="acc")
                for t in range(t0, t0 + per_bank):
                    product(
                        acc[:, t - t0, :],
                        w3_mx,
                        t,
                        z2_mx[0][:, first : first + count],
                        z2_mx[1][:, first : first + count],
                    )
                banks.append(acc)
            return banks

        def finish(first, count, banks):
            last = first + count == S
            per_bank = 2 if last else 512 // count
            res_sb = res_lo if first < 512 else res_hi
            col = first % 512
            result = keep.tile([P, 4, count], F32, name=f"result{first}")
            for b, acc in enumerate(banks):
                rows = slice(b * per_bank, (b + 1) * per_bank)
                nc.vector.tensor_tensor(result[:, rows, :], acc[:], res_sb[:, rows, col : col + count], ADD)
                queue = nc.scalar if b and last else nc.sync
                queue.dma_start(out=out_view[:, rows, first : first + count], in_=result[:, rows, :])

        woven = {}
        banks = {}
        n_chunks = len(OUT_CHUNKS)
        for step in range(n_chunks + 2):
            if step < n_chunks:
                woven[step] = gather_parents(*OUT_CHUNKS[step])
            if 1 <= step <= n_chunks:
                banks[step - 1] = third_layer(*OUT_CHUNKS[step - 1], woven[step - 1])
            if step >= 2:
                finish(*OUT_CHUNKS[step - 2], banks[step - 2])
